import numpy as np
import ml_dtypes


def mxq(x, axis, fmt="e4m3"):
    dtype, down = {"e4m3": (ml_dtypes.float8_e4m3fn, 7), "e5m2": (ml_dtypes.float8_e5m2, 14)}[fmt]
    v = np.moveaxis(np.asarray(x, np.float32).astype(ml_dtypes.bfloat16).astype(np.float64), axis, -1)
    blocks = v.reshape(v.shape[:-1] + (-1, 32))
    amax = np.abs(blocks).max(-1, keepdims=True)
    byte = np.maximum(np.where(amax > 0, np.frexp(amax)[1] - 1 + 127, 0) - down, 1)
    scale = np.exp2(byte - 127.0)
    codes = (blocks / scale).astype(np.float32).astype(dtype).astype(np.float64)
    return np.moveaxis((codes * scale).reshape(v.shape), -1, axis)


WIDE = False


def mx_kscale(k):
    if not WIDE:
        return np.ones(k)
    levels = np.array([10, -10, 5, -5, 0])
    if k % 512:
        return np.exp2(np.random.permutation(np.resize(levels, k // 32))).repeat(32)
    a = np.empty((k // 512, 16))
    for p in range(k // 512):
        a[p, :8] = np.random.permutation(np.resize(levels, 8))
        for g in range(8):
            far = levels[np.abs(levels - a[p, g]) >= 10]
            a[p, g + 8] = far[np.random.randint(len(far))]
    return np.exp2(a.ravel()).repeat(32)


def f64(x):
    return np.asarray(x).astype(np.float64)


def striped(idx):
    return np.tile(idx.reshape(-1, 16).T, (8, 1)).astype(np.uint16)


def unstriped(offs):
    return offs[:16].T.reshape(-1).astype(np.int64)


def striped8(idx):
    return np.concatenate([v.reshape(-1, 16).T for v in idx]).astype(np.uint16)


def unstriped8(offs):
    return np.stack([offs[16 * g:16 * g + 16].T.reshape(-1) for g in range(8)]).astype(np.int64)


E2M1 = np.array([0.0, 0.5, 1.0, 1.5, 2.0, 3.0, 4.0, 6.0, -0.0, -0.5, -1.0, -1.5, -2.0, -3.0, -4.0, -6.0])


def pack_weight(w, fmt):
    k, n = w.shape
    w = f64(np.asarray(w, np.float32).astype(ml_dtypes.bfloat16)).reshape(k // 32, 32, n)
    amax = np.abs(w).max(1)
    if fmt == "e4m3":
        byte = np.frexp(amax)[1] - 1 + 127 - 7
    else:
        mant, ex = np.frexp(amax / 6.0)
        byte = np.where(mant > 0.5, ex, ex - 1) + 127
    byte = np.clip(np.where(amax > 0, byte, 1), 1, 254)
    scaled = (w * np.exp2(127.0 - byte)[:, None, :]).reshape(k, n).astype(np.float32)
    by_word = np.ascontiguousarray(scaled.reshape(k // 512, 128, 4, n).transpose(0, 1, 3, 2))
    if fmt == "e4m3":
        words = by_word.astype(ml_dtypes.float8_e4m3fn).view(np.uint8)
    else:
        c = by_word.astype(ml_dtypes.float4_e2m1fn).view(np.uint8) & 0xF
        words = (c[..., 0::2] | (c[..., 1::2] << 4)).reshape(k // 512, 128, 2 * n)
    return np.ascontiguousarray(words), np.ascontiguousarray(byte.astype(np.uint8).reshape(k // 512, 16, n))


def unpack_weight(words, scales, fmt):
    g, _, n = scales.shape
    words = np.ascontiguousarray(words).reshape(g, 128, n, -1)
    if fmt == "e4m3":
        vals = words.view(ml_dtypes.float8_e4m3fn).astype(np.float64)
    else:
        nib = np.empty((g, 128, n, 4), np.uint8)
        nib[..., 0::2] = words & 0xF
        nib[..., 1::2] = words >> 4
        vals = E2M1[nib]
    vals = vals * np.repeat(np.exp2(scales.astype(np.float64) - 127.0), 8, axis=1)[..., None]
    return vals.transpose(0, 1, 3, 2).reshape(g * 512, n)


def pack_table(v):
    words, scales = pack_weight(v, "e4m3")
    return np.concatenate([words.reshape(words.shape[0], -1), scales.reshape(scales.shape[0], -1)], axis=1)


def unpack_table(tab):
    g, t = tab.shape[0], tab.shape[1] // 528
    return unpack_weight(tab[:, :512 * t].reshape(g, 128, t, 4), tab[:, 512 * t:].reshape(g, 16, t), "e4m3")


K, M, T, S = 512, 512, 1024, 512


def setup_inputs():
    n = np.random.standard_normal
    s = mx_kscale(K)[:, None]
    return {
        "tab": pack_table(n((K, T)) * s),
        "w": (n((K, M)) / np.sqrt(K) / s).astype(np.float32),
        "wgo": np.repeat(np.random.uniform(0.5, 2.0, (8, S)), 16, axis=0).astype(np.float32),
        "offs": striped(np.random.permutation(T)[:S]),
        "offs2": striped8(np.stack([np.random.permutation(T)[:S] for _ in range(8)])),
    }


def reference(tab, w, wgo, offs, offs2):
    tab_ = unpack_table(tab)[:, unstriped(offs)]
    w_ = mxq(f64(w), 0, "e4m3")
    y = w_.T @ tab_
    place = unstriped8(offs2)[np.arange(M) % 128 // 16]
    out = np.zeros((M, T))
    out[np.arange(M)[:, None], place] = f64(wgo)[np.arange(M) % 128] * (y)
    return out

@@ -1,0 +1,104 @@
+from contextlib import ExitStack
+
+import concourse.mybir as mybir
+
+K, M, T, S = 512, 512, 1024, 512
+FLOPS = 2 * K * M * S
+
+F32 = mybir.dt.float32
+BF16 = mybir.dt.bfloat16
+I32 = mybir.dt.int32
+U32 = mybir.dt.uint32
+U16 = mybir.dt.uint16
+U8 = mybir.dt.uint8
+FP8X4 = mybir.dt.float8_e4m3fn_x4
+
+P = 128
+PACK = 4
+M_TILES = M // P
+HALF = S // 2
+LIST_COLS = S // 16
+HALF_COLS = LIST_COLS // 2
+
+
+def tile_list_tabhs_none_kernel(tc, tab, w, wgo, offs, offs2, out):
+    nc = tc.nc
+    mult = mybir.AluOpType.mult
+
+    tab_words = tab[0, 0 : 4 * P * T].rearrange("(p n) -> p n", p=P)
+    tab_scales = tab[0, 4 * P * T :].rearrange("(q n) -> q n", q=16)
+    w_rows = w.rearrange("(p j) c -> p j c", j=PACK)
+
+    with ExitStack() as ctx:
+        lists = ctx.enter_context(tc.tile_pool(name="lists", bufs=1))
+        keep = ctx.enter_context(tc.tile_pool(name="keep", bufs=1))
+        psum = ctx.enter_context(tc.psum_pool(name="psum", bufs=1))
+
+        pick = lists.tile([P, LIST_COLS], U16, name="pick")
+        place = lists.tile([P, LIST_COLS], U16, name="place")
+
+        words = keep.tile([P, T], U32, name="words", align_bytes=64)
+        scales = keep.tile([P, T], U8, name="scales", align_bytes=64)
+        weights_of_place = keep.tile([P, S], F32, name="weights_of_place", align_bytes=64)
+
+        nc.vector.memset(scales[:].bitcast(I32), 0)
+        nc.sync.dma_start(pick[:], offs)
+        for quad in range(4):
+            nc.sync.dma_start(
+                out=scales[32 * quad : 32 * quad + 4, :].bitcast(I32),
+                in_=tab_scales[4 * quad : 4 * quad + 4, :].bitcast(I32),
+            )
+
+        w_raw0 = keep.tile([P, PACK, P], F32, name="w_raw0", align_bytes=64)
+        w_raw_rest = keep.tile([P, PACK, M - P], F32, name="w_raw_rest", align_bytes=64)
+        nc.sync.dma_start(out=words[:].bitcast(I32), in_=tab_words.bitcast(I32))
+        nc.sync.dma_start(out=w_raw0[:], in_=w_rows[:, :, 0:P])
+        nc.sync.dma_start(place[:], offs2)
+        nc.sync.dma_start(out=weights_of_place[:], in_=wgo)
+        nc.sync.dma_start(out=w_raw_rest[:], in_=w_rows[:, :, P:M])
+
+        windows = []
+        for m in range(M_TILES):
+            window = keep.tile([P, T], F32, name=f"window{m}", align_bytes=64)
+            nc.vector.memset(window[:], 0.0)
+            windows.append(window)
+
+        picked_scales = keep.tile([P, S], U8, name="picked_scales", align_bytes=64)
+        nc.vector.tensor_copy(picked_scales[:], scales[:].indirect(pick[:]))
+        picked_words = []
+        for h in range(2):
+            half = keep.tile([P, HALF], U32, name=f"picked_words{h}", align_bytes=64)
+            nc.vector.tensor_copy(half[:], words[:].indirect(pick[:, h * HALF_COLS : (h + 1) * HALF_COLS]))
+            picked_words.append(half)
+
+        for m in range(M_TILES):
+            w_grouped = keep.tile([P, P, PACK], BF16, name=f"w_grouped{m}", align_bytes=64)
+            raw = w_raw0[:] if m == 0 else w_raw_rest[:, :, (m - 1) * P : m * P]
+            nc.scalar.copy(w_grouped[:], raw.rearrange("p j c -> p c j"))
+            w_codes = keep.tile([P, P], U32, name=f"w_codes{m}", align_bytes=64)
+            w_scales = keep.tile([P, P], U8, name=f"w_scales{m}", align_bytes=64)
+            nc.vector.quantize_mx(
+                out=w_codes[:].bitcast(FP8X4),
+                scales=w_scales[:],
+                in_=w_grouped[:].rearrange("p c j -> p (c j)"),
+            )
+            for h in range(2):
+                bank = psum.tile([P, HALF], F32, name=f"bank{m}_{h}")
+                nc.tensor.matmul_mx(
+                    out=bank[:],
+                    lhsT=w_codes[:].bitcast(FP8X4),
+                    lhsT_scale=w_scales[:],
+                    rhs=picked_words[h][:].bitcast(FP8X4),
+                    rhs_scale=picked_scales[:, h * HALF : (h + 1) * HALF],
+                    start=True,
+                    stop=True,
+                )
+                y = keep.tile([P, HALF], F32, name=f"y{m}_{h}", align_bytes=64)
+                nc.scalar.copy(y[:], bank[:])
+                nc.vector.tensor_tensor(
+                    windows[m][:].indirect(place[:, h * HALF_COLS : (h + 1) * HALF_COLS]),
+                    y[:],
+                    weights_of_place[:, h * HALF : (h + 1) * HALF],
+                    mult,
+                )
+            nc.sync.dma_start(out=out[m * P : (m + 1) * P, :], in_=windows[m][:])

@@ -41,55 +41,61 @@ def tile_list_tabhs_none_kernel(tc, tab, w, wgo, offs, offs2, out):
         scales = keep.tile([P, T], U8, name="scales", align_bytes=64)
         weights_of_place = keep.tile([P, S], F32, name="weights_of_place", align_bytes=64)
 
-        nc.vector.memset(scales[:].bitcast(I32), 0)
+        nc.gpsimd.memset(scales[:].bitcast(I32), 0)
+        nc.gpsimd.dma_start(out=weights_of_place[:], in_=wgo)
         nc.sync.dma_start(pick[:], offs)
         for quad in range(4):
             nc.sync.dma_start(
                 out=scales[32 * quad : 32 * quad + 4, :].bitcast(I32),
                 in_=tab_scales[4 * quad : 4 * quad + 4, :].bitcast(I32),
             )
-
-        w_raw0 = keep.tile([P, PACK, P], F32, name="w_raw0", align_bytes=64)
-        w_raw_rest = keep.tile([P, PACK, M - P], F32, name="w_raw_rest", align_bytes=64)
+        w_raw_0 = keep.tile([P, PACK, 1 * P], F32, name="w_raw_0", align_bytes=64)
+        nc.scalar.dma_start(out=w_raw_0[:], in_=w_rows[:, :, 0 * P : 1 * P])
         nc.sync.dma_start(out=words[:].bitcast(I32), in_=tab_words.bitcast(I32))
-        nc.sync.dma_start(out=w_raw0[:], in_=w_rows[:, :, 0:P])
+        w_raw_1 = keep.tile([P, PACK, 3 * P], F32, name="w_raw_1", align_bytes=64)
+        nc.sync.dma_start(out=w_raw_1[:], in_=w_rows[:, :, 1 * P : 4 * P])
         nc.sync.dma_start(place[:], offs2)
-        nc.sync.dma_start(out=weights_of_place[:], in_=wgo)
-        nc.sync.dma_start(out=w_raw_rest[:], in_=w_rows[:, :, P:M])
-
         windows = []
         for m in range(M_TILES):
             window = keep.tile([P, T], F32, name=f"window{m}", align_bytes=64)
-            nc.vector.memset(window[:], 0.0)
+            zero_engine = nc.vector if m < 2 else nc.gpsimd
+            zero_engine.memset(window[:], 0.0)
             windows.append(window)
 
-        picked_scales = keep.tile([P, S], U8, name="picked_scales", align_bytes=64)
-        nc.vector.tensor_copy(picked_scales[:], scales[:].indirect(pick[:]))
-        picked_words = []
-        for h in range(2):
-            half = keep.tile([P, HALF], U32, name=f"picked_words{h}", align_bytes=64)
-            nc.vector.tensor_copy(half[:], words[:].indirect(pick[:, h * HALF_COLS : (h + 1) * HALF_COLS]))
-            picked_words.append(half)
-
-        for m in range(M_TILES):
-            w_grouped = keep.tile([P, P, PACK], BF16, name=f"w_grouped{m}", align_bytes=64)
-            raw = w_raw0[:] if m == 0 else w_raw_rest[:, :, (m - 1) * P : m * P]
-            nc.scalar.copy(w_grouped[:], raw.rearrange("p j c -> p c j"))
-            w_codes = keep.tile([P, P], U32, name=f"w_codes{m}", align_bytes=64)
-            w_scales = keep.tile([P, P], U8, name=f"w_scales{m}", align_bytes=64)
+        def quantize_w(m, raw):
+            grouped = keep.tile([P, P, PACK], BF16, name=f"w_grouped{m}", align_bytes=64)
+            nc.scalar.copy(grouped[:], raw.rearrange("p j c -> p c j"))
+            codes = keep.tile([P, P], U32, name=f"w_codes{m}", align_bytes=64)
+            code_scales = keep.tile([P, P], U8, name=f"w_scales{m}", align_bytes=64)
             nc.vector.quantize_mx(
-                out=w_codes[:].bitcast(FP8X4),
-                scales=w_scales[:],
-                in_=w_grouped[:].rearrange("p c j -> p (c j)"),
+                out=codes[:].bitcast(FP8X4),
+                scales=code_scales[:],
+                in_=grouped[:].rearrange("p c j -> p (c j)"),
             )
+            return codes, code_scales
+
+        halves = [pick[:, h * HALF_COLS : (h + 1) * HALF_COLS] for h in range(2)]
+        picked_scales = [keep.tile([P, HALF], U8, name=f"picked_scales{h}", align_bytes=64) for h in range(2)]
+        picked_words = [keep.tile([P, HALF], U32, name=f"picked_words{h}", align_bytes=64) for h in range(2)]
+        w_tiles = []
+        w_tiles.append(quantize_w(0, w_raw_0[:]))
+        nc.vector.tensor_copy(picked_scales[0][:], scales[:].indirect(halves[0]))
+        nc.vector.tensor_copy(picked_words[0][:], words[:].indirect(halves[0]))
+        nc.vector.tensor_copy(picked_scales[1][:], scales[:].indirect(halves[1]))
+        nc.vector.tensor_copy(picked_words[1][:], words[:].indirect(halves[1]))
+        w_tiles.append(quantize_w(1, w_raw_1[:, :, 0:P]))
+        w_tiles.append(quantize_w(2, w_raw_1[:, :, P : 2 * P]))
+        w_tiles.append(quantize_w(3, w_raw_1[:, :, 2 * P : 3 * P]))
+        for m in range(M_TILES):
+            codes, code_scales = w_tiles[m]
             for h in range(2):
                 bank = psum.tile([P, HALF], F32, name=f"bank{m}_{h}")
                 nc.tensor.matmul_mx(
                     out=bank[:],
-                    lhsT=w_codes[:].bitcast(FP8X4),
-                    lhsT_scale=w_scales[:],
+                    lhsT=codes[:].bitcast(FP8X4),
+                    lhsT_scale=code_scales[:],
                     rhs=picked_words[h][:].bitcast(FP8X4),
-                    rhs_scale=picked_scales[:, h * HALF : (h + 1) * HALF],
+                    rhs_scale=picked_scales[h][:],
                     start=True,
                     stop=True,
                 )

from contextlib import ExitStack

import concourse.mybir as mybir

K, M, T, S = 512, 512, 1024, 512
FLOPS = 2 * K * M * S

F32 = mybir.dt.float32
BF16 = mybir.dt.bfloat16
I32 = mybir.dt.int32
U32 = mybir.dt.uint32
U16 = mybir.dt.uint16
U8 = mybir.dt.uint8
FP8X4 = mybir.dt.float8_e4m3fn_x4

P = 128
PACK = 4
M_TILES = M // P
HALF = S // 2
LIST_COLS = S // 16
HALF_COLS = LIST_COLS // 2


def tile_list_tabhs_none_kernel(tc, tab, w, wgo, offs, offs2, out):
    nc = tc.nc
    mult = mybir.AluOpType.mult

    tab_words = tab[0, 0 : 4 * P * T].rearrange("(p n) -> p n", p=P)
    tab_scales = tab[0, 4 * P * T :].rearrange("(q n) -> q n", q=16)
    w_rows = w.rearrange("(p j) c -> p j c", j=PACK)

    with ExitStack() as ctx:
        lists = ctx.enter_context(tc.tile_pool(name="lists", bufs=1))
        keep = ctx.enter_context(tc.tile_pool(name="keep", bufs=1))
        psum = ctx.enter_context(tc.psum_pool(name="psum", bufs=1))

        pick = lists.tile([P, LIST_COLS], U16, name="pick")
        place = lists.tile([P, LIST_COLS], U16, name="place")

        words = keep.tile([P, T], U32, name="words", align_bytes=64)
        scales = keep.tile([P, T], U8, name="scales", align_bytes=64)
        weights_of_place = keep.tile([P, S], F32, name="weights_of_place", align_bytes=64)

        nc.gpsimd.memset(scales[:].bitcast(I32), 0)
        nc.gpsimd.dma_start(out=weights_of_place[:], in_=wgo)
        nc.sync.dma_start(pick[:], offs)
        for quad in range(4):
            nc.sync.dma_start(
                out=scales[32 * quad : 32 * quad + 4, :].bitcast(I32),
                in_=tab_scales[4 * quad : 4 * quad + 4, :].bitcast(I32),
            )
        w_raw_0 = keep.tile([P, PACK, 1 * P], F32, name="w_raw_0", align_bytes=64)
        nc.scalar.dma_start(out=w_raw_0[:], in_=w_rows[:, :, 0 * P : 1 * P])
        nc.sync.dma_start(out=words[:].bitcast(I32), in_=tab_words.bitcast(I32))
        w_raw_1 = keep.tile([P, PACK, 3 * P], F32, name="w_raw_1", align_bytes=64)
        nc.sync.dma_start(out=w_raw_1[:], in_=w_rows[:, :, 1 * P : 4 * P])
        nc.sync.dma_start(place[:], offs2)
        windows = []
        for m in range(M_TILES):
            window = keep.tile([P, T], F32, name=f"window{m}", align_bytes=64)
            zero_engine = nc.vector if m < 2 else nc.gpsimd
            zero_engine.memset(window[:], 0.0)
            windows.append(window)

        def quantize_w(m, raw):
            grouped = keep.tile([P, P, PACK], BF16, name=f"w_grouped{m}", align_bytes=64)
            nc.scalar.copy(grouped[:], raw.rearrange("p j c -> p c j"))
            codes = keep.tile([P, P], U32, name=f"w_codes{m}", align_bytes=64)
            code_scales = keep.tile([P, P], U8, name=f"w_scales{m}", align_bytes=64)
            nc.vector.quantize_mx(
                out=codes[:].bitcast(FP8X4),
                scales=code_scales[:],
                in_=grouped[:].rearrange("p c j -> p (c j)"),
            )
            return codes, code_scales

        halves = [pick[:, h * HALF_COLS : (h + 1) * HALF_COLS] for h in range(2)]
        picked_scales = [keep.tile([P, HALF], U8, name=f"picked_scales{h}", align_bytes=64) for h in range(2)]
        picked_words = [keep.tile([P, HALF], U32, name=f"picked_words{h}", align_bytes=64) for h in range(2)]
        w_tiles = []
        w_tiles.append(quantize_w(0, w_raw_0[:]))
        nc.vector.tensor_copy(picked_scales[0][:], scales[:].indirect(halves[0]))
        nc.vector.tensor_copy(picked_words[0][:], words[:].indirect(halves[0]))
        nc.vector.tensor_copy(picked_scales[1][:], scales[:].indirect(halves[1]))
        nc.vector.tensor_copy(picked_words[1][:], words[:].indirect(halves[1]))
        w_tiles.append(quantize_w(1, w_raw_1[:, :, 0:P]))
        w_tiles.append(quantize_w(2, w_raw_1[:, :, P : 2 * P]))
        w_tiles.append(quantize_w(3, w_raw_1[:, :, 2 * P : 3 * P]))
        for m in range(M_TILES):
            codes, code_scales = w_tiles[m]
            for h in range(2):
                bank = psum.tile([P, HALF], F32, name=f"bank{m}_{h}")
                nc.tensor.matmul_mx(
                    out=bank[:],
                    lhsT=codes[:].bitcast(FP8X4),
                    lhsT_scale=code_scales[:],
                    rhs=picked_words[h][:].bitcast(FP8X4),
                    rhs_scale=picked_scales[h][:],
                    start=True,
                    stop=True,
                )
                y = keep.tile([P, HALF], F32, name=f"y{m}_{h}", align_bytes=64)
                nc.scalar.copy(y[:], bank[:])
                nc.vector.tensor_tensor(
                    windows[m][:].indirect(place[:, h * HALF_COLS : (h + 1) * HALF_COLS]),
                    y[:],
                    weights_of_place[:, h * HALF : (h + 1) * HALF],
                    mult,
                )
            nc.sync.dma_start(out=out[m * P : (m + 1) * P, :], in_=windows[m][:])
